import numpy as np
import ml_dtypes


def mxq(x, axis, fmt="e4m3"):
    dtype, down = {"e4m3": (ml_dtypes.float8_e4m3fn, 7), "e5m2": (ml_dtypes.float8_e5m2, 14)}[fmt]
    v = np.moveaxis(np.asarray(x, np.float32).astype(ml_dtypes.bfloat16).astype(np.float64), axis, -1)
    blocks = v.reshape(v.shape[:-1] + (-1, 32))
    amax = np.abs(blocks).max(-1, keepdims=True)
    byte = np.maximum(np.where(amax > 0, np.frexp(amax)[1] - 1 + 127, 0) - down, 1)
    scale = np.exp2(byte - 127.0)
    codes = (blocks / scale).astype(np.float32).astype(dtype).astype(np.float64)
    return np.moveaxis((codes * scale).reshape(v.shape), -1, axis)


WIDE = False


def mx_kscale(k):
    if not WIDE:
        return np.ones(k)
    levels = np.array([10, -10, 5, -5, 0])
    if k % 512:
        return np.exp2(np.random.permutation(np.resize(levels, k // 32))).repeat(32)
    a = np.empty((k // 512, 16))
    for p in range(k // 512):
        a[p, :8] = np.random.permutation(np.resize(levels, 8))
        for g in range(8):
            far = levels[np.abs(levels - a[p, g]) >= 10]
            a[p, g + 8] = far[np.random.randint(len(far))]
    return np.exp2(a.ravel()).repeat(32)


def f64(x):
    return np.asarray(x).astype(np.float64)


def striped(idx):
    return np.tile(idx.reshape(-1, 16).T, (8, 1)).astype(np.uint16)


def unstriped(offs):
    return offs[:16].T.reshape(-1).astype(np.int64)


E2M1 = np.array([0.0, 0.5, 1.0, 1.5, 2.0, 3.0, 4.0, 6.0, -0.0, -0.5, -1.0, -1.5, -2.0, -3.0, -4.0, -6.0])


def pack_weight(w, fmt):
    k, n = w.shape
    w = f64(np.asarray(w, np.float32).astype(ml_dtypes.bfloat16)).reshape(k // 32, 32, n)
    amax = np.abs(w).max(1)
    if fmt == "e4m3":
        byte = np.frexp(amax)[1] - 1 + 127 - 7
    else:
        mant, ex = np.frexp(amax / 6.0)
        byte = np.where(mant > 0.5, ex, ex - 1) + 127
    byte = np.clip(np.where(amax > 0, byte, 1), 1, 254)
    scaled = (w * np.exp2(127.0 - byte)[:, None, :]).reshape(k, n).astype(np.float32)
    by_word = np.ascontiguousarray(scaled.reshape(k // 512, 128, 4, n).transpose(0, 1, 3, 2))
    if fmt == "e4m3":
        words = by_word.astype(ml_dtypes.float8_e4m3fn).view(np.uint8)
    else:
        c = by_word.astype(ml_dtypes.float4_e2m1fn).view(np.uint8) & 0xF
        words = (c[..., 0::2] | (c[..., 1::2] << 4)).reshape(k // 512, 128, 2 * n)
    return np.ascontiguousarray(words), np.ascontiguousarray(byte.astype(np.uint8).reshape(k // 512, 16, n))


def unpack_weight(words, scales, fmt):
    g, _, n = scales.shape
    words = np.ascontiguousarray(words).reshape(g, 128, n, -1)
    if fmt == "e4m3":
        vals = words.view(ml_dtypes.float8_e4m3fn).astype(np.float64)
    else:
        nib = np.empty((g, 128, n, 4), np.uint8)
        nib[..., 0::2] = words & 0xF
        nib[..., 1::2] = words >> 4
        vals = E2M1[nib]
    vals = vals * np.repeat(np.exp2(scales.astype(np.float64) - 127.0), 8, axis=1)[..., None]
    return vals.transpose(0, 1, 3, 2).reshape(g * 512, n)


def gelu(v):
    return 0.5 * v * (1.0 + np.tanh(np.sqrt(2.0 / np.pi) * (v + 0.044715 * v**3)))


def twice(P):
    return np.random.permutation(np.repeat(np.arange(P), 2))


K, H, T, S, P = 1024, 1024, 4096, 1024, 512

def setup_inputs():
    n = np.random.standard_normal
    s = mx_kscale(K)[:, None]
    u = mx_kscale(H)[:, None]
    d = {}
    d["tab_words"], d["tab_scales"] = pack_weight(n((K, T)) * s, "e4m3")
    d["offs"] = striped(np.random.permutation(T)[:S])
    d["pos1"] = striped(np.random.permutation(S)[:P])
    d["pos2"] = striped(np.random.permutation(S)[:P])
    d["pos3"] = striped(twice(P))
    d["w1"] = (0.8 * n((K, H)) / K ** 0.5 / s).astype(np.float32)
    d["gain"] = (np.exp(0.3 * n(H)) * u[:, 0]).astype(np.float32)
    d["w2_words"], d["w2_scales"] = pack_weight(0.6 * n((H, H)) / H ** 0.5 / u, "e2m1")
    d["base"] = (1.2 * n((H, P))).astype(np.float32)
    d["keep"] = (np.exp(0.4 * n(H)) / u[:, 0]).astype(np.float32)
    return d

def reference(tab_words, tab_scales, offs, pos1, pos2, pos3, w1, gain, w2_words, w2_scales, base, keep):
    v = unpack_weight(tab_words, tab_scales, "e4m3")[:, unstriped(offs)]
    lin = mxq(f64(w1), 0, "e4m3").T @ v
    h = f64(gain)[:, None] * np.exp(lin)
    z = np.maximum(h[:, unstriped(pos1)], h[:, unstriped(pos2)])
    w2 = unpack_weight(w2_words, w2_scales, "e2m1")
    y = (w2.T @ mxq(z, 0, "e4m3")) + f64(base)
    up = y[:, unstriped(pos3)]
    share = 1.0 / (1.0 + np.exp(-up))
    return share * (f64(keep)[:, None] * h)

@@ -1,0 +1,264 @@
+from contextlib import ExitStack
+
+import concourse.mybir as mybir
+
+K, H, T, S, NC = 1024, 1024, 4096, 1024, 512
+FLOPS = 2 * K * H * S + 2 * H * H * NC
+
+F32 = mybir.dt.float32
+BF16 = mybir.dt.bfloat16
+I32 = mybir.dt.int32
+U32 = mybir.dt.uint32
+U16 = mybir.dt.uint16
+U8 = mybir.dt.uint8
+FP8X4 = mybir.dt.float8_e4m3fn_x4
+FP4X4 = mybir.dt.float4_e2m1fn_x4
+ACT = mybir.ActivationFunctionType
+ALU = mybir.AluOpType
+
+P = 128
+PACK = 4
+PASS = P * PACK
+NPASS = 2
+BANK = 512
+SPARE = 16
+VEC_SHARE = 88
+NWIN = 3
+
+
+def tile_list_catchment_sample_scores_kernel(
+    tc, tab_words, tab_scales, offs, pos1, pos2, pos3, w1, gain, w2_words, w2_scales, base, keep, out
+):
+    nc = tc.nc
+    with ExitStack() as ctx:
+        held = ctx.enter_context(tc.tile_pool(name="held", bufs=1))
+        ring = ctx.enter_context(tc.tile_pool(name="ring", bufs=2))
+        outs = ctx.enter_context(tc.tile_pool(name="outs", bufs=4))
+        psum = ctx.enter_context(tc.psum_pool(name="psum", bufs=1))
+
+        banks = [psum.tile([P, BANK], F32, name="bank%d" % i) for i in range(8)]
+
+        offs_t = held.tile([P, S // 16], U16, name="offs_t")
+        pos1_t = held.tile([P, NC // 16], U16, name="pos1_t")
+        pos2_t = held.tile([P, NC // 16], U16, name="pos2_t")
+        pos3_t = held.tile([P, S // 16], U16, name="pos3_t")
+        tabw = [held.tile([P, T], I32, name="tabw%d" % a, align_bytes=64) for a in range(NPASS)]
+        tabs = held.tile([P, T], U8, name="tabs", align_bytes=64)
+        raw = [[held.tile([P, PACK, PASS], F32, name="raw%d%d" % (b, a)) for a in range(NPASS)] for b in range(2)]
+        gain_t = held.tile([P, 2, PACK], F32, name="gain_t")
+        keep_t = held.tile([P, 2, PACK], F32, name="keep_t")
+        half_keep = held.tile([P, 2, PACK], F32, name="half_keep")
+        w2s_raw = held.tile([P, NPASS * H], U8, name="w2s_raw", align_bytes=64)
+        w2w_raw = held.tile([P, NPASS, H // 2], I32, name="w2w_raw", align_bytes=64)
+        w2s = held.tile([P, NPASS * H], U8, name="w2s", align_bytes=64)
+        w2w = held.tile([P, NPASS * H * 2], U8, name="w2w", align_bytes=64)
+        base_t = [held.tile([P, PACK, NC], F32, name="base%d" % b) for b in range(2)]
+        wins = [held.tile([P, NC + SPARE], F32, name="win%d" % i) for i in range(NWIN)]
+        warm = held.tile([P, 2], F32, name="warm")
+
+        nc.vector.memset(tabs[:].bitcast(I32), 0)
+        nc.vector.memset(w2s_raw[:].bitcast(I32), 0)
+        nc.gpsimd.memset(warm[:, 0:1], 0.0)
+        nc.scalar.activation(warm[:, 1:2], warm[:, 0:1], ACT.Exp)
+        for win in wins:
+            nc.gpsimd.memset(win[:, NC:], 0.0)
+
+        def load_w1(b, a):
+            rows = w1[a * PASS : (a + 1) * PASS, b * PASS : (b + 1) * PASS]
+            nc.sync.dma_start(raw[b][a][:], rows.rearrange("(p j) c -> p j c", j=PACK))
+
+        def load_tab(a):
+            nc.sync.dma_start(tabw[a][:], tab_words[a].rearrange("p t i -> p (t i)").bitcast(I32))
+
+        nc.sync.dma_start(offs_t[:], offs)
+        load_tab(0)
+        for q in range(4):
+            nc.sync.dma_start(
+                tabs[32 * q : 32 * q + 8, :].bitcast(I32), tab_scales[:, 4 * q : 4 * q + 4, :].bitcast(I32)
+            )
+        load_tab(1)
+        load_w1(0, 0)
+        nc.sync.dma_start(pos1_t[:], pos1)
+        nc.sync.dma_start(pos2_t[:], pos2)
+        nc.sync.dma_start(gain_t[:], gain.rearrange("(b p t) -> p b t", b=2, t=PACK))
+        load_w1(0, 1)
+        load_w1(1, 0)
+        for q in range(4):
+            nc.sync.dma_start(
+                w2s_raw[32 * q : 32 * q + 4, :].bitcast(I32).rearrange("r (a n) -> r a n", a=NPASS),
+                w2_scales[:, 4 * q : 4 * q + 4, :].bitcast(I32).rearrange("a r n -> r a n"),
+            )
+        nc.sync.dma_start(w2w_raw[:], w2_words.bitcast(I32).rearrange("a p n -> p a n"))
+        load_w1(1, 1)
+        nc.sync.dma_start(pos3_t[:], pos3)
+        nc.sync.dma_start(keep_t[:], keep.rearrange("(b p t) -> p b t", b=2, t=PACK))
+        for b in range(2):
+            nc.sync.dma_start(base_t[b][:], base[b * PASS : (b + 1) * PASS, :].rearrange("(p t) m -> p t m", t=PACK))
+
+        vw = [held.tile([P, S], U32, name="vw%d" % a, align_bytes=64) for a in range(NPASS)]
+        vs = held.tile([P, S], U8, name="vs", align_bytes=64)
+        nc.vector.tensor_copy(vw[0][:], tabw[0][:].bitcast(U32).indirect(offs_t[:]))
+        nc.vector.tensor_copy(vs[:], tabs[:].indirect(offs_t[:]))
+        nc.vector.tensor_copy(vw[1][:], tabw[1][:].bitcast(U32).indirect(offs_t[:]))
+
+        wq = [[held.tile([P, PASS], U32, name="wq%d%d" % (b, a), align_bytes=64) for a in range(NPASS)] for b in range(2)]
+        wsc = [[held.tile([P, PASS], U8, name="wsc%d%d" % (b, a), align_bytes=64) for a in range(NPASS)] for b in range(2)]
+        grouped = {}
+
+        def round_w1(b, a, vec_m):
+            wb = ring.tile([P, PACK * PASS], BF16, name="wb", align_bytes=64)
+            grouped[(b, a)] = wb
+            dst = wb[:].rearrange("p (t m j) -> p m j t", t=PACK, j=PACK)
+            src = raw[b][a][:].rearrange("p j (m t) -> p m j t", t=PACK)
+            if vec_m > 0:
+                nc.vector.tensor_copy(dst[:, 0:vec_m], src[:, 0:vec_m])
+            if vec_m < P:
+                nc.scalar.copy(dst[:, vec_m:P], src[:, vec_m:P])
+
+        def quantise_w1(b, a):
+            wb = grouped[(b, a)]
+            for t in range(PACK):
+                cols = slice(t * P, (t + 1) * P)
+                nc.vector.quantize_mx(
+                    wq[b][a][:, cols].bitcast(FP8X4), wsc[b][a][:, cols], wb[:, t * PASS : (t + 1) * PASS]
+                )
+
+        def first_pass(b, t, a):
+            cols = slice(t * P, (t + 1) * P)
+            for half in range(2):
+                js = slice(half * BANK, (half + 1) * BANK)
+                nc.tensor.matmul_mx(
+                    banks[2 * t + half][:],
+                    lhsT=wq[b][a][:, cols].bitcast(FP8X4),
+                    lhsT_scale=wsc[b][a][:, cols],
+                    rhs=vw[a][:, js].bitcast(FP8X4),
+                    rhs_scale=vs[4 * a : P, js],
+                    start=(a == 0),
+                    stop=(a == NPASS - 1),
+                )
+
+        h = [[held.tile([P, S], F32, name="h%d%d" % (b, t)) for t in range(PACK)] for b in range(2)]
+
+        def features(b, t):
+            e = ring.tile([P, S], F32, name="e")
+            for half in range(2):
+                js = slice(half * BANK, (half + 1) * BANK)
+                nc.scalar.activation(e[:, js], banks[2 * t + half][:], ACT.Exp)
+            nc.scalar.activation(h[b][t][:], e[:], ACT.Copy, scale=gain_t[:, b, t : t + 1])
+
+        pick1 = held.tile([P, PACK, NC], F32, name="pick1")
+        pick2 = held.tile([P, PACK, NC], F32, name="pick2")
+
+        def pick(b, t):
+            nc.vector.tensor_copy(pick1[:, t, :], h[b][t][:].indirect(pos1_t[:]))
+            nc.vector.tensor_copy(pick2[:, t, :], h[b][t][:].indirect(pos2_t[:]))
+
+        zb = [held.tile([P, NC * PACK], BF16, name="zb%d" % b, align_bytes=64) for b in range(2)]
+        zq = [held.tile([P, NC], U32, name="zq%d" % b, align_bytes=64) for b in range(2)]
+        zs = [held.tile([P, NC], U8, name="zs%d" % b, align_bytes=64) for b in range(2)]
+
+        def larger(b, half):
+            cs = slice(half * NC // 8, (half + 1) * NC // 8)
+            nc.vector.tensor_tensor(
+                zb[b][:].rearrange("p (c i t) -> p c t i", i=4, t=PACK)[:, cs],
+                pick1[:].rearrange("p t (c i) -> p c t i", i=4)[:, cs],
+                pick2[:].rearrange("p t (c i) -> p c t i", i=4)[:, cs],
+                ALU.max,
+            )
+
+        def quantise_z(b, half):
+            ms = slice(half * NC // 2, (half + 1) * NC // 2)
+            nc.vector.quantize_mx(
+                zq[b][:, ms].bitcast(FP8X4), zs[b][:, ms], zb[b][:, half * NC * 2 : (half + 1) * NC * 2]
+            )
+
+        def deal_w2():
+            nc.vector.tensor_copy(
+                w2s[:].rearrange("p (g t m) -> p g m t", t=PACK, m=P),
+                w2s_raw[:].rearrange("p (g m t) -> p g m t", t=PACK, m=P),
+            )
+            nc.vector.tensor_copy(
+                w2w[:].bitcast(U16).rearrange("p (g t m) -> p g m t", t=PACK, m=P),
+                w2w_raw[:].rearrange("p a n -> p (a n)").bitcast(U16).rearrange("p (g m t) -> p g m t", t=PACK, m=P),
+            )
+
+        round_w1(0, 0, P)
+        quantise_w1(0, 0)
+        for t in range(PACK):
+            first_pass(0, t, 0)
+        round_w1(0, 1, VEC_SHARE)
+        quantise_w1(0, 1)
+        for t in range(PACK):
+            first_pass(0, t, 1)
+        features(0, 0)
+        pick(0, 0)
+        features(0, 1)
+        pick(0, 1)
+        round_w1(1, 0, 0)
+        deal_w2()
+        quantise_w1(1, 0)
+        features(0, 2)
+        pick(0, 2)
+        features(0, 3)
+        pick(0, 3)
+        round_w1(1, 1, 0)
+        larger(0, 0)
+        quantise_w1(1, 1)
+        larger(0, 1)
+        quantise_z(0, 0)
+        quantise_z(0, 1)
+        for t in range(PACK):
+            for a in range(NPASS):
+                first_pass(1, t, a)
+            features(1, t)
+            pick(1, t)
+        nc.scalar.activation(half_keep[:], keep_t[:], ACT.Copy, scale=0.5)
+
+        def second_pass(i, a):
+            c0 = a * H + i * P
+            nc.tensor.matmul_mx(
+                banks[i][:],
+                lhsT=w2w[:, 2 * c0 : 2 * (c0 + P)].bitcast(FP4X4),
+                lhsT_scale=w2s[:, c0 : c0 + P],
+                rhs=zq[a][:].bitcast(FP8X4),
+                rhs_scale=zs[a][:],
+                start=(a == 0),
+                stop=(a == NPASS - 1),
+            )
+
+        for i in range(8):
+            second_pass(i, 0)
+        larger(1, 0)
+        larger(1, 1)
+        quantise_z(1, 0)
+        quantise_z(1, 1)
+        for i in range(8):
+            second_pass(i, 1)
+
+        out_rows = out.rearrange("(b p t) j -> b t p j", b=2, t=PACK)
+
+        def scores(i):
+            b, t = divmod(i, PACK)
+            y = outs.tile([P, NC], F32, name="y")
+            nc.vector.tensor_tensor(y[:], banks[i][:], base_t[b][:, t, :], ALU.add)
+            th = ring.tile([P, NC], F32, name="th")
+            nc.scalar.activation(th[:], y[:], ACT.Tanh, scale=0.5)
+            hk = half_keep[:, b, t : t + 1]
+            nc.scalar.activation(wins[i % NWIN][:, 0:NC], th[:], ACT.Identity, bias=hk, scale=hk)
+
+        def weigh(i):
+            b, t = divmod(i, PACK)
+            for half in range(2):
+                js = slice(half * BANK, (half + 1) * BANK)
+                res = outs.tile([P, BANK], F32, name="res")
+                nc.vector.tensor_tensor(
+                    res[:], wins[i % NWIN][:].indirect(pos3_t[:, 32 * half : 32 * (half + 1)]), h[b][t][:, js], ALU.mult
+                )
+                nc.sync.dma_start(out_rows[b, t, :, js], res[:])
+
+        scores(0)
+        scores(1)
+        for i in range(8):
+            if i + 2 < 8:
+                scores(i + 2)
+            weigh(i)

@@ -1,6 +1,7 @@
 from contextlib import ExitStack
 
 import concourse.mybir as mybir
+from concourse.masks import make_identity
 
 K, H, T, S, NC = 1024, 1024, 4096, 1024, 512
 FLOPS = 2 * K * H * S + 2 * H * H * NC
@@ -22,8 +23,7 @@ PASS = P * PACK
 NPASS = 2
 BANK = 512
 SPARE = 16
-VEC_SHARE = 88
-NWIN = 3
+NWIN = 4
 
 
 def tile_list_catchment_sample_scores_kernel(
@@ -42,123 +42,123 @@ def tile_list_catchment_sample_scores_kernel(
         pos1_t = held.tile([P, NC // 16], U16, name="pos1_t")
         pos2_t = held.tile([P, NC // 16], U16, name="pos2_t")
         pos3_t = held.tile([P, S // 16], U16, name="pos3_t")
-        tabw = [held.tile([P, T], I32, name="tabw%d" % a, align_bytes=64) for a in range(NPASS)]
-        tabs = held.tile([P, T], U8, name="tabs", align_bytes=64)
-        raw = [[held.tile([P, PACK, PASS], F32, name="raw%d%d" % (b, a)) for a in range(NPASS)] for b in range(2)]
-        gain_t = held.tile([P, 2, PACK], F32, name="gain_t")
-        keep_t = held.tile([P, 2, PACK], F32, name="keep_t")
-        half_keep = held.tile([P, 2, PACK], F32, name="half_keep")
-        w2s_raw = held.tile([P, NPASS * H], U8, name="w2s_raw", align_bytes=64)
-        w2w_raw = held.tile([P, NPASS, H // 2], I32, name="w2w_raw", align_bytes=64)
-        w2s = held.tile([P, NPASS * H], U8, name="w2s", align_bytes=64)
-        w2w = held.tile([P, NPASS * H * 2], U8, name="w2w", align_bytes=64)
-        base_t = [held.tile([P, PACK, NC], F32, name="base%d" % b) for b in range(2)]
+        gain_t = held.tile([P, 2 * PACK], F32, name="gain_t")
+        keep_t = held.tile([P, 2 * PACK], F32, name="keep_t")
+        kg = held.tile([P, 2 * PACK], F32, name="kg")
+        half_kg = held.tile([P, 2 * PACK], F32, name="half_kg")
+        gain_rows = held.tile([P, 2 * PACK * NC], F32, name="gain_rows")
+        ident = held.tile([P, P], F32, name="ident")
         wins = [held.tile([P, NC + SPARE], F32, name="win%d" % i) for i in range(NWIN)]
         warm = held.tile([P, 2], F32, name="warm")
 
-        nc.vector.memset(tabs[:].bitcast(I32), 0)
-        nc.vector.memset(w2s_raw[:].bitcast(I32), 0)
-        nc.gpsimd.memset(warm[:, 0:1], 0.0)
+        def shared(shape, dtype, name, tag):
+            return held.tile(shape, dtype, name=name, tag=tag, align_bytes=64)
+
+        tabw = [shared([P, T], I32, "tabw%d" % a, "words%d" % a) for a in range(NPASS)]
+        tabs = shared([P, T], U8, "tabs", "scales")
+        vs_spread = shared([P, S], U8, "vs_spread", "spread")
+        vs = held.tile([P, NPASS * S], U8, name="vs", align_bytes=64)
+
+        nc.gpsimd.memset(tabs[:, T // 2 :].bitcast(I32), 0)
+        nc.vector.memset(tabs[:, : T // 2].bitcast(I32), 0)
+        nc.vector.memset(warm[:, 0:1], 0.0)
         nc.scalar.activation(warm[:, 1:2], warm[:, 0:1], ACT.Exp)
+        nc.vector.memset(vs[:].bitcast(I32), 0)
         for win in wins:
-            nc.gpsimd.memset(win[:, NC:], 0.0)
+            nc.vector.memset(win[:, NC:], 0.0)
+        make_identity(nc, ident[:])
 
-        def load_w1(b, a):
+        raw = {}
+
+        def load_w1(b, a, tag):
+            raw[(b, a)] = shared([P, PACK, PASS], F32, "raw%d%d" % (b, a), tag)
             rows = w1[a * PASS : (a + 1) * PASS, b * PASS : (b + 1) * PASS]
-            nc.sync.dma_start(raw[b][a][:], rows.rearrange("(p j) c -> p j c", j=PACK))
+            nc.sync.dma_start(raw[(b, a)][:], rows.rearrange("(p j) c -> p j c", j=PACK))
 
-        def load_tab(a):
-            nc.sync.dma_start(tabw[a][:], tab_words[a].rearrange("p t i -> p (t i)").bitcast(I32))
+        def load_tab(a, c0, c1):
+            nc.sync.dma_start(tabw[a][:, c0:c1], tab_words[a].rearrange("p t i -> p (t i)").bitcast(I32)[:, c0:c1])
 
         nc.sync.dma_start(offs_t[:], offs)
-        load_tab(0)
-        for q in range(4):
-            nc.sync.dma_start(
-                tabs[32 * q : 32 * q + 8, :].bitcast(I32), tab_scales[:, 4 * q : 4 * q + 4, :].bitcast(I32)
-            )
-        load_tab(1)
-        load_w1(0, 0)
+        load_tab(0, 0, T // 2)
         nc.sync.dma_start(pos1_t[:], pos1)
         nc.sync.dma_start(pos2_t[:], pos2)
-        nc.sync.dma_start(gain_t[:], gain.rearrange("(b p t) -> p b t", b=2, t=PACK))
-        load_w1(0, 1)
-        load_w1(1, 0)
-        for q in range(4):
-            nc.sync.dma_start(
-                w2s_raw[32 * q : 32 * q + 4, :].bitcast(I32).rearrange("r (a n) -> r a n", a=NPASS),
-                w2_scales[:, 4 * q : 4 * q + 4, :].bitcast(I32).rearrange("a r n -> r a n"),
-            )
-        nc.sync.dma_start(w2w_raw[:], w2_words.bitcast(I32).rearrange("a p n -> p a n"))
-        load_w1(1, 1)
         nc.sync.dma_start(pos3_t[:], pos3)
-        nc.sync.dma_start(keep_t[:], keep.rearrange("(b p t) -> p b t", b=2, t=PACK))
-        for b in range(2):
-            nc.sync.dma_start(base_t[b][:], base[b * PASS : (b + 1) * PASS, :].rearrange("(p t) m -> p t m", t=PACK))
+        nc.sync.dma_start(gain_t[:].rearrange("p (b t) -> p b t", b=2), gain.rearrange("(b p t) -> p b t", b=2, t=PACK))
+        nc.sync.dma_start(tabs[0:P:4, :].bitcast(I32), tab_scales.bitcast(I32).rearrange("a q n -> q a n"))
+        load_tab(0, T // 2, T)
+        load_tab(1, 0, T)
+        nc.sync.dma_start(keep_t[:].rearrange("p (b t) -> p b t", b=2), keep.rearrange("(b p t) -> p b t", b=2, t=PACK))
+        for i in range(2 * PACK):
+            nc.scalar.copy(gain_rows[:, i * NC : (i + 1) * NC], gain_t[:, i : i + 1].to_broadcast([P, NC]))
+        nc.gpsimd.tensor_tensor(kg[:], keep_t[:], gain_t[:], ALU.mult)
+        nc.gpsimd.tensor_scalar(half_kg[:], kg[:], 0.5, 0.0, ALU.mult, ALU.add)
 
         vw = [held.tile([P, S], U32, name="vw%d" % a, align_bytes=64) for a in range(NPASS)]
-        vs = held.tile([P, S], U8, name="vs", align_bytes=64)
+        nc.vector.tensor_copy(vs_spread[:], tabs[:].indirect(offs_t[:]))
+        for q in range(4):
+            nc.sync.dma_start(
+                vs[32 * q : 32 * q + 4, :].bitcast(I32).rearrange("r (a n) -> r a n", a=NPASS),
+                vs_spread[32 * q : 32 * q + 32 : 4, :].bitcast(I32),
+            )
+        load_w1(0, 0, "scales")
         nc.vector.tensor_copy(vw[0][:], tabw[0][:].bitcast(U32).indirect(offs_t[:]))
-        nc.vector.tensor_copy(vs[:], tabs[:].indirect(offs_t[:]))
+        load_w1(0, 1, "words0")
         nc.vector.tensor_copy(vw[1][:], tabw[1][:].bitcast(U32).indirect(offs_t[:]))
+        load_w1(1, 0, "spread")
+        load_w1(1, 1, "words1")
 
-        wq = [[held.tile([P, PASS], U32, name="wq%d%d" % (b, a), align_bytes=64) for a in range(NPASS)] for b in range(2)]
-        wsc = [[held.tile([P, PASS], U8, name="wsc%d%d" % (b, a), align_bytes=64) for a in range(NPASS)] for b in range(2)]
-        grouped = {}
+        wq = [held.tile([P, NPASS * PASS], U32, name="wq%d" % b, align_bytes=64) for b in range(2)]
+        wsc = [held.tile([P, NPASS * PASS], U8, name="wsc%d" % b, align_bytes=64) for b in range(2)]
+        wb = [shared([P, NPASS * PACK * PASS], BF16, "wb%d" % b, "wb%d" % b) for b in range(2)]
 
-        def round_w1(b, a, vec_m):
-            wb = ring.tile([P, PACK * PASS], BF16, name="wb", align_bytes=64)
-            grouped[(b, a)] = wb
-            dst = wb[:].rearrange("p (t m j) -> p m j t", t=PACK, j=PACK)
-            src = raw[b][a][:].rearrange("p j (m t) -> p m j t", t=PACK)
-            if vec_m > 0:
-                nc.vector.tensor_copy(dst[:, 0:vec_m], src[:, 0:vec_m])
-            if vec_m < P:
-                nc.scalar.copy(dst[:, vec_m:P], src[:, vec_m:P])
+        def round_w1(b, a, copy, ts, ms):
+            dst = wb[b][:].rearrange("p (t a m j) -> p a m j t", t=PACK, a=NPASS, j=PACK)[:, a]
+            src = raw[(b, a)][:].rearrange("p j (m t) -> p m j t", t=PACK)
+            copy(dst[:, ms, :, ts], src[:, ms, :, ts])
 
-        def quantise_w1(b, a):
-            wb = grouped[(b, a)]
-            for t in range(PACK):
-                cols = slice(t * P, (t + 1) * P)
-                nc.vector.quantize_mx(
-                    wq[b][a][:, cols].bitcast(FP8X4), wsc[b][a][:, cols], wb[:, t * PASS : (t + 1) * PASS]
-                )
+        def quantise_w1(b, u0, u1):
+            cols = slice(u0 * P, u1 * P)
+            nc.vector.quantize_mx(wq[b][:, cols].bitcast(FP8X4), wsc[b][:, cols], wb[b][:, u0 * PASS : u1 * PASS])
 
-        def first_pass(b, t, a):
-            cols = slice(t * P, (t + 1) * P)
+        def first_pass(b, t, half, a):
+            cols = slice((NPASS * t + a) * P, (NPASS * t + a + 1) * P)
+            nc.tensor.matmul_mx(
+                banks[2 * t + half][:],
+                lhsT=wq[b][:, cols].bitcast(FP8X4),
+                lhsT_scale=wsc[b][:, cols],
+                rhs=vw[a][:, half * BANK : (half + 1) * BANK].bitcast(FP8X4),
+                rhs_scale=vs[:, a * S + half * BANK : a * S + (half + 1) * BANK],
+                start=(a == 0),
+                stop=(a == NPASS - 1),
+            )
+
+        def first_product(b, t):
             for half in range(2):
-                js = slice(half * BANK, (half + 1) * BANK)
-                nc.tensor.matmul_mx(
-                    banks[2 * t + half][:],
-                    lhsT=wq[b][a][:, cols].bitcast(FP8X4),
-                    lhsT_scale=wsc[b][a][:, cols],
-                    rhs=vw[a][:, js].bitcast(FP8X4),
-                    rhs_scale=vs[4 * a : P, js],
-                    start=(a == 0),
-                    stop=(a == NPASS - 1),
-                )
+                for a in range(NPASS):
+                    first_pass(b, t, half, a)
 
-        h = [[held.tile([P, S], F32, name="h%d%d" % (b, t)) for t in range(PACK)] for b in range(2)]
+        e = [[held.tile([P, S], F32, name="e%d%d" % (b, t)) for t in range(PACK)] for b in range(2)]
 
         def features(b, t):
-            e = ring.tile([P, S], F32, name="e")
             for half in range(2):
                 js = slice(half * BANK, (half + 1) * BANK)
-                nc.scalar.activation(e[:, js], banks[2 * t + half][:], ACT.Exp)
-            nc.scalar.activation(h[b][t][:], e[:], ACT.Copy, scale=gain_t[:, b, t : t + 1])
+                nc.scalar.activation(e[b][t][:, js], banks[2 * t + half][:], ACT.Exp)
 
         pick1 = held.tile([P, PACK, NC], F32, name="pick1")
         pick2 = held.tile([P, PACK, NC], F32, name="pick2")
 
         def pick(b, t):
-            nc.vector.tensor_copy(pick1[:, t, :], h[b][t][:].indirect(pos1_t[:]))
-            nc.vector.tensor_copy(pick2[:, t, :], h[b][t][:].indirect(pos2_t[:]))
+            i = PACK * b + t
+            g = gain_rows[:, i * NC : (i + 1) * NC]
+            nc.vector.tensor_tensor(pick1[:, t, :], e[b][t][:].indirect(pos1_t[:]), g, ALU.mult)
+            nc.vector.tensor_tensor(pick2[:, t, :], e[b][t][:].indirect(pos2_t[:]), g, ALU.mult)
 
-        zb = [held.tile([P, NC * PACK], BF16, name="zb%d" % b, align_bytes=64) for b in range(2)]
+        zb = {}
         zq = [held.tile([P, NC], U32, name="zq%d" % b, align_bytes=64) for b in range(2)]
         zs = [held.tile([P, NC], U8, name="zs%d" % b, align_bytes=64) for b in range(2)]
 
-        def larger(b, half):
-            cs = slice(half * NC // 8, (half + 1) * NC // 8)
+        def larger(b, m0, m1):
+            cs = slice(m0 // 4, m1 // 4)
             nc.vector.tensor_tensor(
                 zb[b][:].rearrange("p (c i t) -> p c t i", i=4, t=PACK)[:, cs],
                 pick1[:].rearrange("p t (c i) -> p c t i", i=4)[:, cs],
@@ -166,99 +166,183 @@ def tile_list_catchment_sample_scores_kernel(
                 ALU.max,
             )
 
-        def quantise_z(b, half):
-            ms = slice(half * NC // 2, (half + 1) * NC // 2)
-            nc.vector.quantize_mx(
-                zq[b][:, ms].bitcast(FP8X4), zs[b][:, ms], zb[b][:, half * NC * 2 : (half + 1) * NC * 2]
-            )
+        def quantise_z(b, m0, m1):
+            nc.vector.quantize_mx(zq[b][:, m0:m1].bitcast(FP8X4), zs[b][:, m0:m1], zb[b][:, PACK * m0 : PACK * m1])
 
-        def deal_w2():
-            nc.vector.tensor_copy(
-                w2s[:].rearrange("p (g t m) -> p g m t", t=PACK, m=P),
-                w2s_raw[:].rearrange("p (g m t) -> p g m t", t=PACK, m=P),
-            )
-            nc.vector.tensor_copy(
-                w2w[:].bitcast(U16).rearrange("p (g t m) -> p g m t", t=PACK, m=P),
-                w2w_raw[:].rearrange("p a n -> p (a n)").bitcast(U16).rearrange("p (g m t) -> p g m t", t=PACK, m=P),
-            )
+        every = slice(0, P)
+        round_w1(0, 0, nc.scalar.copy, slice(0, 1), every)
+        round_w1(0, 0, nc.scalar.copy, slice(1, 2), every)
+        round_w1(0, 0, nc.vector.tensor_copy, slice(2, PACK), every)
+        quantise_w1(0, 0, 1)
+        for half in range(2):
+            first_pass(0, 0, half, 0)
+        round_w1(0, 1, nc.vector.tensor_copy, slice(0, 1), every)
+        round_w1(0, 1, nc.scalar.copy, slice(1, 2), every)
+        quantise_w1(0, 1, 2)
+        for half in range(2):
+            first_pass(0, 0, half, 1)
+        round_w1(0, 1, nc.vector.tensor_copy, slice(2, PACK), every)
+        quantise_w1(0, 2, 4)
+        quantise_w1(0, 4, 8)
+        for t in range(1, PACK):
+            first_product(0, t)
 
-        round_w1(0, 0, P)
-        quantise_w1(0, 0)
+        base_t = [shared([P, PACK, NC], F32, "base0", "scales"), shared([P, PACK, NC], F32, "base1", "words0")]
+        w2w = shared([P, NPASS * H * 2], U8, "w2w", "wb0")
+        nc.sync.dma_start(base_t[0][:], base[0:PASS, :].rearrange("(p t) m -> p t m", t=PACK))
+        nc.sync.dma_start(
+            w2w[:].bitcast(I32).rearrange("p (a n) -> p a n", a=NPASS), w2_words.bitcast(I32).rearrange("a p n -> p a n")
+        )
+        nc.sync.dma_start(base_t[1][:], base[PASS:H, :].rearrange("(p t) m -> p t m", t=PACK))
+
         for t in range(PACK):
-            first_pass(0, t, 0)
-        round_w1(0, 1, VEC_SHARE)
-        quantise_w1(0, 1)
+            features(0, t)
+            pick(0, t)
+        for a in range(NPASS):
+            for m0 in range(0, P, P // 2):
+                round_w1(1, a, nc.scalar.copy, slice(0, PACK), slice(m0, m0 + P // 2))
+        w2s = shared([P, NPASS * H], U8, "w2s", "spread")
+        nc.gpsimd.memset(w2s[:].bitcast(I32), 0)
+        for q in range(4):
+            nc.sync.dma_start(
+                w2s[32 * q : 32 * q + 4, :].bitcast(I32).rearrange("r (a n) -> r a n", a=NPASS),
+                w2_scales[:, 4 * q : 4 * q + 4, :].bitcast(I32).rearrange("a r n -> r a n"),
+            )
+        quantise_w1(1, 0, 4)
+        quantise_w1(1, 4, 8)
+        zb[0] = shared([P, NC * PACK], BF16, "zb0", "wb1")
+        zb[1] = shared([P, NC * PACK], BF16, "zb1", "zb1")
+        larger(0, 0, NC // 2)
+        larger(0, NC // 2, NC)
+        quantise_z(0, 0, NC // 2)
+        quantise_z(0, NC // 2, NC)
         for t in range(PACK):
-            first_pass(0, t, 1)
-        features(0, 0)
-        pick(0, 0)
-        features(0, 1)
-        pick(0, 1)
-        round_w1(1, 0, 0)
-        deal_w2()
-        quantise_w1(1, 0)
-        features(0, 2)
-        pick(0, 2)
-        features(0, 3)
-        pick(0, 3)
-        round_w1(1, 1, 0)
-        larger(0, 0)
-        quantise_w1(1, 1)
-        larger(0, 1)
-        quantise_z(0, 0)
-        quantise_z(0, 1)
-        for t in range(PACK):
-            for a in range(NPASS):
-                first_pass(1, t, a)
+            first_product(1, t)
             features(1, t)
             pick(1, t)
-        nc.scalar.activation(half_keep[:], keep_t[:], ACT.Copy, scale=0.5)
 
-        def second_pass(i, a):
-            c0 = a * H + i * P
+        base_turned = [held.tile([P, PACK * NC], F32, name="base_turned%d" % b) for b in range(2)]
+        y_turned = [held.tile([P, PACK * PASS], F32, name="y_turned%d" % b) for b in range(2)]
+
+        def turn_base(b, t):
+            bank = banks[4 + t if b == 0 else t]
+            for mt in range(4):
+                nc.tensor.transpose(bank[:, mt * P : (mt + 1) * P], base_t[b][:, t, mt * P : (mt + 1) * P], ident[:])
+            nc.scalar.copy(base_turned[b][:, t * NC : (t + 1) * NC], bank[:])
+
+        def second_pass(b, mt, a):
+            c0 = a * H + b * PASS
+            ms = slice(mt * P, (mt + 1) * P)
             nc.tensor.matmul_mx(
-                banks[i][:],
-                lhsT=w2w[:, 2 * c0 : 2 * (c0 + P)].bitcast(FP4X4),
-                lhsT_scale=w2s[:, c0 : c0 + P],
-                rhs=zq[a][:].bitcast(FP8X4),
-                rhs_scale=zs[a][:],
+                banks[4 + mt][:],
+                lhsT=zq[a][:, ms].bitcast(FP8X4),
+                lhsT_scale=zs[a][:, ms],
+                rhs=w2w[:, 2 * c0 : 2 * (c0 + PASS)].bitcast(FP4X4),
+                rhs_scale=w2s[:, c0 : c0 + PASS],
                 start=(a == 0),
                 stop=(a == NPASS - 1),
             )
 
-        for i in range(8):
-            second_pass(i, 0)
-        larger(1, 0)
-        larger(1, 1)
-        quantise_z(1, 0)
-        quantise_z(1, 1)
-        for i in range(8):
-            second_pass(i, 1)
+        def leave_bank(b, mt, t0, t1):
+            nc.scalar.copy(
+                y_turned[b][:, mt * PASS : (mt + 1) * PASS].rearrange("m (t p) -> m t p", t=PACK)[:, t0:t1],
+                banks[4 + mt][:].rearrange("m (p t) -> m t p", t=PACK)[:, t0:t1],
+            )
+
+        def sum_parts(i):
+            return [(banks[0], 0, 3), (banks[3], 3, 4)] if i == 0 else [(banks[i % PACK], 0, 4)]
+
+        def add_base(i):
+            b, t = divmod(i, PACK)
+            for bank, mt0, mt1 in sum_parts(i):
+                for mt in range(mt0, mt1):
+                    c0 = t * NC + mt * P
+                    nc.tensor.matmul(
+                        bank[:, mt * P : (mt + 1) * P],
+                        lhsT=base_turned[b][:, c0 : c0 + P],
+                        rhs=ident[:],
+                        start=(mt == mt0),
+                        stop=False,
+                        is_transpose=True,
+                    )
+
+        def add_y(i, mt):
+            b, t = divmod(i, PACK)
+            c0 = mt * PASS + t * P
+            for bank, mt0, mt1 in sum_parts(i):
+                if mt0 <= mt < mt1:
+                    nc.tensor.matmul(
+                        bank[:, mt * P : (mt + 1) * P],
+                        lhsT=y_turned[b][:, c0 : c0 + P],
+                        rhs=ident[:],
+                        start=False,
+                        stop=(mt == mt1 - 1),
+                        is_transpose=True,
+                    )
+
+        def share(i, part):
+            bank, mt0, mt1 = sum_parts(i)[part]
+            ms = slice(mt0 * P, mt1 * P)
+            th = ring.tile([P, NC], F32, name="th")
+            nc.scalar.activation(th[:, ms], bank[:, ms], ACT.Tanh, scale=0.5)
+            hk = half_kg[:, i : i + 1]
+            nc.scalar.activation(wins[i % NWIN][:, ms], th[:, ms], ACT.Identity, bias=hk, scale=hk)
 
         out_rows = out.rearrange("(b p t) j -> b t p j", b=2, t=PACK)
 
-        def scores(i):
+        def weigh(i, cuts):
             b, t = divmod(i, PACK)
-            y = outs.tile([P, NC], F32, name="y")
-            nc.vector.tensor_tensor(y[:], banks[i][:], base_t[b][:, t, :], ALU.add)
-            th = ring.tile([P, NC], F32, name="th")
-            nc.scalar.activation(th[:], y[:], ACT.Tanh, scale=0.5)
-            hk = half_keep[:, b, t : t + 1]
-            nc.scalar.activation(wins[i % NWIN][:, 0:NC], th[:], ACT.Identity, bias=hk, scale=hk)
-
-        def weigh(i):
-            b, t = divmod(i, PACK)
-            for half in range(2):
-                js = slice(half * BANK, (half + 1) * BANK)
+            for j0, j1 in zip(cuts[:-1], cuts[1:]):
                 res = outs.tile([P, BANK], F32, name="res")
                 nc.vector.tensor_tensor(
-                    res[:], wins[i % NWIN][:].indirect(pos3_t[:, 32 * half : 32 * (half + 1)]), h[b][t][:, js], ALU.mult
+                    res[:, 0 : j1 - j0],
+                    wins[i % NWIN][:].indirect(pos3_t[:, j0 // 16 : j1 // 16]),
+                    e[b][t][:, j0:j1],
+                    ALU.mult,
                 )
-                nc.sync.dma_start(out_rows[b, t, :, js], res[:])
+                nc.sync.dma_start(out_rows[b, t, :, j0:j1], res[:, 0 : j1 - j0])
 
-        scores(0)
-        scores(1)
-        for i in range(8):
-            if i + 2 < 8:
-                scores(i + 2)
-            weigh(i)
+        for t in range(PACK):
+            turn_base(0, t)
+        for mt in range(4):
+            second_pass(0, mt, 0)
+        for i in range(PACK - 1):
+            add_base(i)
+        larger(1, 0, P)
+        for mt in range(4):
+            if mt < 3:
+                larger(1, (mt + 1) * P, (mt + 2) * P)
+            quantise_z(1, mt * P, (mt + 1) * P)
+            second_pass(0, mt, 1)
+            leave_bank(0, mt, 0, 1)
+            add_y(0, mt)
+            if mt >= 2:
+                share(0, mt - 2)
+        for mt in range(4):
+            leave_bank(0, mt, 1, 2)
+            add_y(1, mt)
+        share(1, 0)
+        weigh(0, [0, BANK, S])
+        for mt in range(4):
+            leave_bank(0, mt, 2, PACK)
+            add_y(2, mt)
+        share(2, 0)
+        weigh(1, [0, BANK, S])
+        add_base(3)
+        for mt in range(4):
+            add_y(3, mt)
+        for mt in range(4):
+            second_pass(1, mt, 0)
+            second_pass(1, mt, 1)
+        share(3, 0)
+        weigh(2, [0, BANK, S])
+        for mt in range(4):
+            leave_bank(1, mt, 0, PACK)
+        for i in range(PACK, 2 * PACK):
+            turn_base(1, i - PACK)
+            add_base(i)
+            for mt in range(4):
+                add_y(i, mt)
+            share(i, 0)
+            weigh(i - 1, [0, BANK, S])
+        weigh(2 * PACK - 1, [0, BANK, BANK + BANK // 2, S])

from contextlib import ExitStack

import concourse.mybir as mybir
from concourse.masks import make_identity

K, H, T, S, NC = 1024, 1024, 4096, 1024, 512
FLOPS = 2 * K * H * S + 2 * H * H * NC

F32 = mybir.dt.float32
BF16 = mybir.dt.bfloat16
I32 = mybir.dt.int32
U32 = mybir.dt.uint32
U16 = mybir.dt.uint16
U8 = mybir.dt.uint8
FP8X4 = mybir.dt.float8_e4m3fn_x4
FP4X4 = mybir.dt.float4_e2m1fn_x4
ACT = mybir.ActivationFunctionType
ALU = mybir.AluOpType

P = 128
PACK = 4
PASS = P * PACK
NPASS = 2
BANK = 512
SPARE = 16
NWIN = 4


def tile_list_catchment_sample_scores_kernel(
    tc, tab_words, tab_scales, offs, pos1, pos2, pos3, w1, gain, w2_words, w2_scales, base, keep, out
):
    nc = tc.nc
    with ExitStack() as ctx:
        held = ctx.enter_context(tc.tile_pool(name="held", bufs=1))
        ring = ctx.enter_context(tc.tile_pool(name="ring", bufs=2))
        outs = ctx.enter_context(tc.tile_pool(name="outs", bufs=4))
        psum = ctx.enter_context(tc.psum_pool(name="psum", bufs=1))

        banks = [psum.tile([P, BANK], F32, name="bank%d" % i) for i in range(8)]

        offs_t = held.tile([P, S // 16], U16, name="offs_t")
        pos1_t = held.tile([P, NC // 16], U16, name="pos1_t")
        pos2_t = held.tile([P, NC // 16], U16, name="pos2_t")
        pos3_t = held.tile([P, S // 16], U16, name="pos3_t")
        gain_t = held.tile([P, 2 * PACK], F32, name="gain_t")
        keep_t = held.tile([P, 2 * PACK], F32, name="keep_t")
        kg = held.tile([P, 2 * PACK], F32, name="kg")
        half_kg = held.tile([P, 2 * PACK], F32, name="half_kg")
        gain_rows = held.tile([P, 2 * PACK * NC], F32, name="gain_rows")
        ident = held.tile([P, P], F32, name="ident")
        wins = [held.tile([P, NC + SPARE], F32, name="win%d" % i) for i in range(NWIN)]
        warm = held.tile([P, 2], F32, name="warm")

        def shared(shape, dtype, name, tag):
            return held.tile(shape, dtype, name=name, tag=tag, align_bytes=64)

        tabw = [shared([P, T], I32, "tabw%d" % a, "words%d" % a) for a in range(NPASS)]
        tabs = shared([P, T], U8, "tabs", "scales")
        vs_spread = shared([P, S], U8, "vs_spread", "spread")
        vs = held.tile([P, NPASS * S], U8, name="vs", align_bytes=64)

        nc.gpsimd.memset(tabs[:, T // 2 :].bitcast(I32), 0)
        nc.vector.memset(tabs[:, : T // 2].bitcast(I32), 0)
        nc.vector.memset(warm[:, 0:1], 0.0)
        nc.scalar.activation(warm[:, 1:2], warm[:, 0:1], ACT.Exp)
        nc.vector.memset(vs[:].bitcast(I32), 0)
        for win in wins:
            nc.vector.memset(win[:, NC:], 0.0)
        make_identity(nc, ident[:])

        raw = {}

        def load_w1(b, a, tag):
            raw[(b, a)] = shared([P, PACK, PASS], F32, "raw%d%d" % (b, a), tag)
            rows = w1[a * PASS : (a + 1) * PASS, b * PASS : (b + 1) * PASS]
            nc.sync.dma_start(raw[(b, a)][:], rows.rearrange("(p j) c -> p j c", j=PACK))

        def load_tab(a, c0, c1):
            nc.sync.dma_start(tabw[a][:, c0:c1], tab_words[a].rearrange("p t i -> p (t i)").bitcast(I32)[:, c0:c1])

        nc.sync.dma_start(offs_t[:], offs)
        load_tab(0, 0, T // 2)
        nc.sync.dma_start(pos1_t[:], pos1)
        nc.sync.dma_start(pos2_t[:], pos2)
        nc.sync.dma_start(pos3_t[:], pos3)
        nc.sync.dma_start(gain_t[:].rearrange("p (b t) -> p b t", b=2), gain.rearrange("(b p t) -> p b t", b=2, t=PACK))
        nc.sync.dma_start(tabs[0:P:4, :].bitcast(I32), tab_scales.bitcast(I32).rearrange("a q n -> q a n"))
        load_tab(0, T // 2, T)
        load_tab(1, 0, T)
        nc.sync.dma_start(keep_t[:].rearrange("p (b t) -> p b t", b=2), keep.rearrange("(b p t) -> p b t", b=2, t=PACK))
        for i in range(2 * PACK):
            nc.scalar.copy(gain_rows[:, i * NC : (i + 1) * NC], gain_t[:, i : i + 1].to_broadcast([P, NC]))
        nc.gpsimd.tensor_tensor(kg[:], keep_t[:], gain_t[:], ALU.mult)
        nc.gpsimd.tensor_scalar(half_kg[:], kg[:], 0.5, 0.0, ALU.mult, ALU.add)

        vw = [held.tile([P, S], U32, name="vw%d" % a, align_bytes=64) for a in range(NPASS)]
        nc.vector.tensor_copy(vs_spread[:], tabs[:].indirect(offs_t[:]))
        for q in range(4):
            nc.sync.dma_start(
                vs[32 * q : 32 * q + 4, :].bitcast(I32).rearrange("r (a n) -> r a n", a=NPASS),
                vs_spread[32 * q : 32 * q + 32 : 4, :].bitcast(I32),
            )
        load_w1(0, 0, "scales")
        nc.vector.tensor_copy(vw[0][:], tabw[0][:].bitcast(U32).indirect(offs_t[:]))
        load_w1(0, 1, "words0")
        nc.vector.tensor_copy(vw[1][:], tabw[1][:].bitcast(U32).indirect(offs_t[:]))
        load_w1(1, 0, "spread")
        load_w1(1, 1, "words1")

        wq = [held.tile([P, NPASS * PASS], U32, name="wq%d" % b, align_bytes=64) for b in range(2)]
        wsc = [held.tile([P, NPASS * PASS], U8, name="wsc%d" % b, align_bytes=64) for b in range(2)]
        wb = [shared([P, NPASS * PACK * PASS], BF16, "wb%d" % b, "wb%d" % b) for b in range(2)]

        def round_w1(b, a, copy, ts, ms):
            dst = wb[b][:].rearrange("p (t a m j) -> p a m j t", t=PACK, a=NPASS, j=PACK)[:, a]
            src = raw[(b, a)][:].rearrange("p j (m t) -> p m j t", t=PACK)
            copy(dst[:, ms, :, ts], src[:, ms, :, ts])

        def quantise_w1(b, u0, u1):
            cols = slice(u0 * P, u1 * P)
            nc.vector.quantize_mx(wq[b][:, cols].bitcast(FP8X4), wsc[b][:, cols], wb[b][:, u0 * PASS : u1 * PASS])

        def first_pass(b, t, half, a):
            cols = slice((NPASS * t + a) * P, (NPASS * t + a + 1) * P)
            nc.tensor.matmul_mx(
                banks[2 * t + half][:],
                lhsT=wq[b][:, cols].bitcast(FP8X4),
                lhsT_scale=wsc[b][:, cols],
                rhs=vw[a][:, half * BANK : (half + 1) * BANK].bitcast(FP8X4),
                rhs_scale=vs[:, a * S + half * BANK : a * S + (half + 1) * BANK],
                start=(a == 0),
                stop=(a == NPASS - 1),
            )

        def first_product(b, t):
            for half in range(2):
                for a in range(NPASS):
                    first_pass(b, t, half, a)

        e = [[held.tile([P, S], F32, name="e%d%d" % (b, t)) for t in range(PACK)] for b in range(2)]

        def features(b, t):
            for half in range(2):
                js = slice(half * BANK, (half + 1) * BANK)
                nc.scalar.activation(e[b][t][:, js], banks[2 * t + half][:], ACT.Exp)

        pick1 = held.tile([P, PACK, NC], F32, name="pick1")
        pick2 = held.tile([P, PACK, NC], F32, name="pick2")

        def pick(b, t):
            i = PACK * b + t
            g = gain_rows[:, i * NC : (i + 1) * NC]
            nc.vector.tensor_tensor(pick1[:, t, :], e[b][t][:].indirect(pos1_t[:]), g, ALU.mult)
            nc.vector.tensor_tensor(pick2[:, t, :], e[b][t][:].indirect(pos2_t[:]), g, ALU.mult)

        zb = {}
        zq = [held.tile([P, NC], U32, name="zq%d" % b, align_bytes=64) for b in range(2)]
        zs = [held.tile([P, NC], U8, name="zs%d" % b, align_bytes=64) for b in range(2)]

        def larger(b, m0, m1):
            cs = slice(m0 // 4, m1 // 4)
            nc.vector.tensor_tensor(
                zb[b][:].rearrange("p (c i t) -> p c t i", i=4, t=PACK)[:, cs],
                pick1[:].rearrange("p t (c i) -> p c t i", i=4)[:, cs],
                pick2[:].rearrange("p t (c i) -> p c t i", i=4)[:, cs],
                ALU.max,
            )

        def quantise_z(b, m0, m1):
            nc.vector.quantize_mx(zq[b][:, m0:m1].bitcast(FP8X4), zs[b][:, m0:m1], zb[b][:, PACK * m0 : PACK * m1])

        every = slice(0, P)
        round_w1(0, 0, nc.scalar.copy, slice(0, 1), every)
        round_w1(0, 0, nc.scalar.copy, slice(1, 2), every)
        round_w1(0, 0, nc.vector.tensor_copy, slice(2, PACK), every)
        quantise_w1(0, 0, 1)
        for half in range(2):
            first_pass(0, 0, half, 0)
        round_w1(0, 1, nc.vector.tensor_copy, slice(0, 1), every)
        round_w1(0, 1, nc.scalar.copy, slice(1, 2), every)
        quantise_w1(0, 1, 2)
        for half in range(2):
            first_pass(0, 0, half, 1)
        round_w1(0, 1, nc.vector.tensor_copy, slice(2, PACK), every)
        quantise_w1(0, 2, 4)
        quantise_w1(0, 4, 8)
        for t in range(1, PACK):
            first_product(0, t)

        base_t = [shared([P, PACK, NC], F32, "base0", "scales"), shared([P, PACK, NC], F32, "base1", "words0")]
        w2w = shared([P, NPASS * H * 2], U8, "w2w", "wb0")
        nc.sync.dma_start(base_t[0][:], base[0:PASS, :].rearrange("(p t) m -> p t m", t=PACK))
        nc.sync.dma_start(
            w2w[:].bitcast(I32).rearrange("p (a n) -> p a n", a=NPASS), w2_words.bitcast(I32).rearrange("a p n -> p a n")
        )
        nc.sync.dma_start(base_t[1][:], base[PASS:H, :].rearrange("(p t) m -> p t m", t=PACK))

        for t in range(PACK):
            features(0, t)
            pick(0, t)
        for a in range(NPASS):
            for m0 in range(0, P, P // 2):
                round_w1(1, a, nc.scalar.copy, slice(0, PACK), slice(m0, m0 + P // 2))
        w2s = shared([P, NPASS * H], U8, "w2s", "spread")
        nc.gpsimd.memset(w2s[:].bitcast(I32), 0)
        for q in range(4):
            nc.sync.dma_start(
                w2s[32 * q : 32 * q + 4, :].bitcast(I32).rearrange("r (a n) -> r a n", a=NPASS),
                w2_scales[:, 4 * q : 4 * q + 4, :].bitcast(I32).rearrange("a r n -> r a n"),
            )
        quantise_w1(1, 0, 4)
        quantise_w1(1, 4, 8)
        zb[0] = shared([P, NC * PACK], BF16, "zb0", "wb1")
        zb[1] = shared([P, NC * PACK], BF16, "zb1", "zb1")
        larger(0, 0, NC // 2)
        larger(0, NC // 2, NC)
        quantise_z(0, 0, NC // 2)
        quantise_z(0, NC // 2, NC)
        for t in range(PACK):
            first_product(1, t)
            features(1, t)
            pick(1, t)

        base_turned = [held.tile([P, PACK * NC], F32, name="base_turned%d" % b) for b in range(2)]
        y_turned = [held.tile([P, PACK * PASS], F32, name="y_turned%d" % b) for b in range(2)]

        def turn_base(b, t):
            bank = banks[4 + t if b == 0 else t]
            for mt in range(4):
                nc.tensor.transpose(bank[:, mt * P : (mt + 1) * P], base_t[b][:, t, mt * P : (mt + 1) * P], ident[:])
            nc.scalar.copy(base_turned[b][:, t * NC : (t + 1) * NC], bank[:])

        def second_pass(b, mt, a):
            c0 = a * H + b * PASS
            ms = slice(mt * P, (mt + 1) * P)
            nc.tensor.matmul_mx(
                banks[4 + mt][:],
                lhsT=zq[a][:, ms].bitcast(FP8X4),
                lhsT_scale=zs[a][:, ms],
                rhs=w2w[:, 2 * c0 : 2 * (c0 + PASS)].bitcast(FP4X4),
                rhs_scale=w2s[:, c0 : c0 + PASS],
                start=(a == 0),
                stop=(a == NPASS - 1),
            )

        def leave_bank(b, mt, t0, t1):
            nc.scalar.copy(
                y_turned[b][:, mt * PASS : (mt + 1) * PASS].rearrange("m (t p) -> m t p", t=PACK)[:, t0:t1],
                banks[4 + mt][:].rearrange("m (p t) -> m t p", t=PACK)[:, t0:t1],
            )

        def sum_parts(i):
            return [(banks[0], 0, 3), (banks[3], 3, 4)] if i == 0 else [(banks[i % PACK], 0, 4)]

        def add_base(i):
            b, t = divmod(i, PACK)
            for bank, mt0, mt1 in sum_parts(i):
                for mt in range(mt0, mt1):
                    c0 = t * NC + mt * P
                    nc.tensor.matmul(
                        bank[:, mt * P : (mt + 1) * P],
                        lhsT=base_turned[b][:, c0 : c0 + P],
                        rhs=ident[:],
                        start=(mt == mt0),
                        stop=False,
                        is_transpose=True,
                    )

        def add_y(i, mt):
            b, t = divmod(i, PACK)
            c0 = mt * PASS + t * P
            for bank, mt0, mt1 in sum_parts(i):
                if mt0 <= mt < mt1:
                    nc.tensor.matmul(
                        bank[:, mt * P : (mt + 1) * P],
                        lhsT=y_turned[b][:, c0 : c0 + P],
                        rhs=ident[:],
                        start=False,
                        stop=(mt == mt1 - 1),
                        is_transpose=True,
                    )

        def share(i, part):
            bank, mt0, mt1 = sum_parts(i)[part]
            ms = slice(mt0 * P, mt1 * P)
            th = ring.tile([P, NC], F32, name="th")
            nc.scalar.activation(th[:, ms], bank[:, ms], ACT.Tanh, scale=0.5)
            hk = half_kg[:, i : i + 1]
            nc.scalar.activation(wins[i % NWIN][:, ms], th[:, ms], ACT.Identity, bias=hk, scale=hk)

        out_rows = out.rearrange("(b p t) j -> b t p j", b=2, t=PACK)

        def weigh(i, cuts):
            b, t = divmod(i, PACK)
            for j0, j1 in zip(cuts[:-1], cuts[1:]):
                res = outs.tile([P, BANK], F32, name="res")
                nc.vector.tensor_tensor(
                    res[:, 0 : j1 - j0],
                    wins[i % NWIN][:].indirect(pos3_t[:, j0 // 16 : j1 // 16]),
                    e[b][t][:, j0:j1],
                    ALU.mult,
                )
                nc.sync.dma_start(out_rows[b, t, :, j0:j1], res[:, 0 : j1 - j0])

        for t in range(PACK):
            turn_base(0, t)
        for mt in range(4):
            second_pass(0, mt, 0)
        for i in range(PACK - 1):
            add_base(i)
        larger(1, 0, P)
        for mt in range(4):
            if mt < 3:
                larger(1, (mt + 1) * P, (mt + 2) * P)
            quantise_z(1, mt * P, (mt + 1) * P)
            second_pass(0, mt, 1)
            leave_bank(0, mt, 0, 1)
            add_y(0, mt)
            if mt >= 2:
                share(0, mt - 2)
        for mt in range(4):
            leave_bank(0, mt, 1, 2)
            add_y(1, mt)
        share(1, 0)
        weigh(0, [0, BANK, S])
        for mt in range(4):
            leave_bank(0, mt, 2, PACK)
            add_y(2, mt)
        share(2, 0)
        weigh(1, [0, BANK, S])
        add_base(3)
        for mt in range(4):
            add_y(3, mt)
        for mt in range(4):
            second_pass(1, mt, 0)
            second_pass(1, mt, 1)
        share(3, 0)
        weigh(2, [0, BANK, S])
        for mt in range(4):
            leave_bank(1, mt, 0, PACK)
        for i in range(PACK, 2 * PACK):
            turn_base(1, i - PACK)
            add_base(i)
            for mt in range(4):
                add_y(i, mt)
            share(i, 0)
            weigh(i - 1, [0, BANK, S])
        weigh(2 * PACK - 1, [0, BANK, BANK + BANK // 2, S])
